import numpy as np
import ml_dtypes


def mxq(x, axis, fmt="e4m3"):
    dtype, down = {"e4m3": (ml_dtypes.float8_e4m3fn, 7), "e5m2": (ml_dtypes.float8_e5m2, 14)}[fmt]
    v = np.moveaxis(np.asarray(x, np.float32).astype(ml_dtypes.bfloat16).astype(np.float64), axis, -1)
    blocks = v.reshape(v.shape[:-1] + (-1, 32))
    amax = np.abs(blocks).max(-1, keepdims=True)
    byte = np.maximum(np.where(amax > 0, np.frexp(amax)[1] - 1 + 127, 0) - down, 1)
    scale = np.exp2(byte - 127.0)
    codes = (blocks / scale).astype(np.float32).astype(dtype).astype(np.float64)
    return np.moveaxis((codes * scale).reshape(v.shape), -1, axis)


WIDE = False


def mx_kscale(k):
    if not WIDE:
        return np.ones(k)
    levels = np.array([10, -10, 5, -5, 0])
    if k % 512:
        return np.exp2(np.random.permutation(np.resize(levels, k // 32))).repeat(32)
    a = np.empty((k // 512, 16))
    for p in range(k // 512):
        a[p, :8] = np.random.permutation(np.resize(levels, 8))
        for g in range(8):
            far = levels[np.abs(levels - a[p, g]) >= 10]
            a[p, g + 8] = far[np.random.randint(len(far))]
    return np.exp2(a.ravel()).repeat(32)


def f64(x):
    return np.asarray(x).astype(np.float64)


def striped(idx):
    return np.tile(idx.reshape(-1, 16).T, (8, 1)).astype(np.uint16)


def unstriped(offs):
    return offs[:16].T.reshape(-1).astype(np.int64)


def striped8(idx):
    return np.concatenate([x.reshape(-1, 16).T for x in idx]).astype(np.uint16)


def runs(offs, k):
    lists = np.stack([offs[16 * r : 16 * r + 16].T.reshape(-1) for r in range(8)]).astype(np.int64)
    return lists[np.arange(k) % 512 // 64]


def pack_weight(w):
    k, n = w.shape
    w = f64(np.asarray(w, np.float32).astype(ml_dtypes.bfloat16)).reshape(k // 32, 32, n)
    amax = np.abs(w).max(1)
    byte = np.clip(np.where(amax > 0, np.frexp(amax)[1] - 1 + 127 - 7, 1), 1, 254)
    scaled = (w * np.exp2(127.0 - byte)[:, None, :]).reshape(k, n).astype(np.float32)
    words = np.ascontiguousarray(scaled.reshape(k // 512, 128, 4, n).transpose(0, 1, 3, 2)).astype(ml_dtypes.float8_e4m3fn).view(np.uint8)
    return words, np.ascontiguousarray(byte.astype(np.uint8).reshape(k // 512, 16, n))


def unpack_weight(words, scales):
    g, p, n, _ = words.shape
    vals = np.ascontiguousarray(words).view(ml_dtypes.float8_e4m3fn).astype(np.float64) * np.repeat(np.exp2(scales.astype(np.float64) - 127.0), 8, axis=1)[..., None]
    return vals.transpose(0, 1, 3, 2).reshape(g * 512, n)


def sigmoid(v):
    return 1.0 / (1.0 + np.exp(-np.maximum(v, -700.0)))


K, T, S, N, H = 512, 2048, 512, 512, 512


def setup_inputs():
    n = np.random.standard_normal
    s = mx_kscale(K)[:, None]
    u = mx_kscale(H)
    packed_xT = pack_weight(n((K, T)) * s)
    return {
        "x_words": packed_xT[0],
        "x_scales": packed_xT[1],
        "w1": (n((K, H)) / np.sqrt(K) / s).astype(np.float32),
        "gn": (np.random.uniform(0.5, 1.5, (H, 1)) * u[:, None]).astype(np.float32),
        "w2": (n((H, N)) / np.sqrt(H) / u[:, None]).astype(np.float32),
        "offs": striped(np.random.permutation(T)[:S]),
        "pos": striped8(np.stack([np.random.permutation(S) for _ in range(8)])),
        "neg": striped8(np.stack([np.random.permutation(S) for _ in range(8)])),
    }


def reference(x_words, x_scales, w1, gn, w2, offs, pos, neg):
    xq = unpack_weight(x_words, x_scales)[:, unstriped(offs)]
    p = np.clip(sigmoid(mxq(f64(w1), 0, "e4m3").T @ xq), 0.05, 0.95)
    w = -1.0 * (p[np.arange(H)[:, None], runs(pos, H)]) + 1
    z = f64(gn) * (((w) ** 2) * (-1.0 * (np.log(p[np.arange(H)[:, None], runs(pos, H)]))) - (((p[np.arange(H)[:, None], runs(neg, H)]) ** 2) * (-1.0 * (np.log(-1.0 * (p[np.arange(H)[:, None], runs(neg, H)]) + 1)))))
    return mxq(f64(w2), 0, "e4m3").T @ mxq(z, 0, "e4m3")

@@ -1,0 +1,201 @@
+from contextlib import ExitStack
+
+import concourse.mybir as mybir
+
+K, T, S, H, N = 512, 2048, 512, 512, 512
+FLOPS = 2 * K * H * S + 2 * H * N * S
+
+F32 = mybir.dt.float32
+BF16 = mybir.dt.bfloat16
+I32 = mybir.dt.int32
+U32 = mybir.dt.uint32
+U16 = mybir.dt.uint16
+U8 = mybir.dt.uint8
+FP8X4 = mybir.dt.float8_e4m3fn_x4
+ACT = mybir.ActivationFunctionType
+ALU = mybir.AluOpType
+
+P = 128
+PACK = 4
+STRIPE = 16
+QUARTER = S // 4
+OUT_SLICES = ((0, 256), (256, 128), (384, 128))
+
+
+def tile_picked_focalpair_none_p_kernel(
+    tc, x_words, x_scales, w1, gn, w2, offs, pos, neg, out
+):
+    nc = tc.nc
+    with ExitStack() as ctx:
+        lists = ctx.enter_context(tc.tile_pool(name="lists", bufs=1))
+        sb = ctx.enter_context(tc.tile_pool(name="sb", bufs=1))
+        ps = ctx.enter_context(tc.psum_pool(name="ps", bufs=1))
+
+        offs_t = lists.tile([P, S // STRIPE], U16, name="offs_t")
+        pos_t = lists.tile([P, S // STRIPE], U16, name="pos_t")
+        neg_t = lists.tile([P, S // STRIPE], U16, name="neg_t")
+
+        xs_all = sb.tile([P, T], U8, name="xs_all", align_bytes=64)
+        xw_all = sb.tile([P, T], U32, name="xw_all", align_bytes=64)
+        w1_raw = sb.tile([P, PACK, H], F32, name="w1_raw", align_bytes=64)
+        w2_raw = sb.tile([P, PACK, N], F32, name="w2_raw", align_bytes=64)
+        gn_t = sb.tile([P, PACK], F32, name="gn_t", align_bytes=64)
+
+        nc.vector.memset(xs_all[:].bitcast(I32), 0)
+        nc.sync.dma_start(out=w1_raw[:], in_=w1.rearrange("(p j) c -> p j c", j=PACK))
+        nc.sync.dma_start(offs_t[:], offs)
+        for q in range(4):
+            nc.sync.dma_start(
+                out=xs_all[32 * q : 32 * q + 4, :].bitcast(I32),
+                in_=x_scales[0, 4 * q : 4 * q + 4, :].bitcast(I32),
+            )
+        nc.sync.dma_start(
+            out=xw_all[:].bitcast(I32),
+            in_=x_words[0].rearrange("p n r -> p (n r)").bitcast(I32),
+        )
+        nc.sync.dma_start(out=w2_raw[:], in_=w2.rearrange("(p j) c -> p j c", j=PACK))
+        nc.sync.dma_start(out=gn_t[:], in_=gn.rearrange("(p t) o -> p (t o)", t=PACK))
+        nc.sync.dma_start(pos_t[:], pos)
+        nc.sync.dma_start(neg_t[:], neg)
+
+        w1_bf = sb.tile([P, PACK * H], BF16, name="w1_bf", align_bytes=64)
+        w1_dst = w1_bf[:].rearrange("p (t m j) -> p m j t", t=PACK, j=PACK)
+        w1_src = w1_raw[:].rearrange("p j (m t) -> p m j t", t=PACK)
+        nc.vector.tensor_copy(out=w1_dst[:, :80], in_=w1_src[:, :80])
+        nc.scalar.copy(out=w1_dst[:, 80:], in_=w1_src[:, 80:])
+        xs = [sb.tile([P, S // 2], U8, name="xs%d" % h, align_bytes=64) for h in range(2)]
+        nc.vector.tensor_copy(xs[0][:], xs_all[:].indirect(offs_t[:, : S // 2 // STRIPE]))
+        w1_codes = sb.tile([P, H], U32, name="w1_codes", align_bytes=64)
+        w1_scales = sb.tile([P, H], U8, name="w1_scales", align_bytes=64)
+        nc.vector.quantize_mx(out=w1_codes[:].bitcast(FP8X4), scales=w1_scales[:], in_=w1_bf[:])
+
+        raw_p = sb.tile([P, PACK, S], F32, name="raw_p", align_bytes=64)
+        for c in range(4):
+            cols = slice(c * QUARTER, (c + 1) * QUARTER)
+            if c == 2:
+                nc.vector.tensor_copy(xs[1][:], xs_all[:].indirect(offs_t[:, S // 2 // STRIPE :]))
+            xw = sb.tile([P, QUARTER], U32, name="xw%d" % c, align_bytes=64)
+            nc.vector.tensor_copy(
+                xw[:],
+                xw_all[:].indirect(offs_t[:, c * QUARTER // STRIPE : (c + 1) * QUARTER // STRIPE]),
+            )
+            u = ps.tile([P, PACK, QUARTER], F32, name="u%d" % c)
+            for t in range(PACK):
+                nc.tensor.matmul_mx(
+                    out=u[:, t, :],
+                    lhsT=w1_codes[:, t * P : (t + 1) * P].bitcast(FP8X4),
+                    lhsT_scale=w1_scales[:, t * P : (t + 1) * P],
+                    rhs=xw[:].bitcast(FP8X4),
+                    rhs_scale=xs[c // 2][:, (c % 2) * QUARTER : (c % 2 + 1) * QUARTER],
+                    start=True,
+                    stop=True,
+                )
+            nc.scalar.activation(raw_p[:, :, cols], u[:], ACT.Sigmoid)
+        prob = [sb.tile([P, S], F32, name="prob%d" % t, align_bytes=64) for t in range(PACK)]
+        for t in range(PACK):
+            nc.vector.tensor_scalar(prob[t][:], raw_p[:, t, :], 0.05, 0.95, ALU.max, ALU.min)
+
+        w2_bf = sb.tile([P, N, PACK], BF16, name="w2_bf", align_bytes=64)
+        w2_codes = sb.tile([P, N], U32, name="w2_codes", align_bytes=64)
+        w2_scales = sb.tile([P, N], U8, name="w2_scales", align_bytes=64)
+
+        def round_w2():
+            nc.vector.tensor_copy(
+                out=w2_bf[:].rearrange("p (c i) j -> p c j i", i=4),
+                in_=w2_raw[:].rearrange("p j (c i) -> p c j i", i=4),
+            )
+
+        def quantize_w2():
+            nc.vector.quantize_mx(
+                out=w2_codes[:].bitcast(FP8X4),
+                scales=w2_scales[:],
+                in_=w2_bf[:].rearrange("p n j -> p (n j)"),
+            )
+
+        def planes(name):
+            return [sb.tile([P, PACK, n], F32, name="%s%d" % (name, s0), align_bytes=64) for s0, n in OUT_SLICES]
+
+        p_pos, p_neg = planes("p_pos"), planes("p_neg")
+        log_pos, log_neg = planes("log_pos"), planes("log_neg")
+        sq_pos, sq_neg = planes("sq_pos"), planes("sq_neg")
+        at_pos, at_neg = planes("at_pos"), planes("at_neg")
+
+        def fetch_pos(i):
+            s0, n = OUT_SLICES[i]
+            for t in range(PACK):
+                nc.vector.tensor_copy(
+                    p_pos[i][:, t, :], prob[t][:].indirect(pos_t[:, s0 // STRIPE : (s0 + n) // STRIPE])
+                )
+
+        def fetch_neg(i):
+            s0, n = OUT_SLICES[i]
+            for t in range(PACK):
+                nc.scalar.activation(
+                    p_neg[i][:, t, :],
+                    prob[t][:].indirect(neg_t[:, s0 // STRIPE : (s0 + n) // STRIPE]),
+                    ACT.Copy,
+                )
+
+        def losses(i):
+            nc.scalar.activation(log_neg[i][:], p_neg[i][:], ACT.Ln, bias=1.0, scale=-1.0)
+            nc.scalar.activation(log_pos[i][:], p_pos[i][:], ACT.Ln)
+            nc.scalar.activation(sq_pos[i][:], p_pos[i][:], ACT.Square, bias=1.0, scale=-1.0)
+            for t in range(PACK):
+                nc.vector.scalar_tensor_tensor(
+                    sq_neg[i][:, t, :], p_neg[i][:, t, :], gn_t[:, t : t + 1], p_neg[i][:, t, :], ALU.mult, ALU.mult
+                )
+            nc.vector.tensor_tensor(at_neg[i][:], sq_neg[i][:], log_neg[i][:], ALU.mult)
+            for t in range(PACK):
+                nc.vector.scalar_tensor_tensor(
+                    at_pos[i][:, t, :], sq_pos[i][:, t, :], gn_t[:, t : t + 1], log_pos[i][:, t, :], ALU.mult, ALU.mult
+                )
+
+        def second_product(i):
+            s0, n = OUT_SLICES[i]
+            z = sb.tile([P, n, PACK], BF16, name="z%d" % s0, align_bytes=64)
+            nc.vector.tensor_tensor(
+                z[:].rearrange("p (c i) t -> p c t i", i=2),
+                at_neg[i][:].rearrange("p t (c i) -> p c t i", i=2),
+                at_pos[i][:].rearrange("p t (c i) -> p c t i", i=2),
+                ALU.subtract,
+            )
+            z_codes = sb.tile([P, n], U32, name="z_codes%d" % s0, align_bytes=64)
+            z_scales = sb.tile([P, n], U8, name="z_scales%d" % s0, align_bytes=64)
+            nc.vector.quantize_mx(
+                out=z_codes[:].bitcast(FP8X4),
+                scales=z_scales[:],
+                in_=z[:].rearrange("p n t -> p (n t)"),
+            )
+            per_bank = 512 // n
+            for b in range(PACK // per_bank):
+                acc = ps.tile([P, per_bank, n], F32, name="acc%d_%d" % (s0, b))
+                for a in range(per_bank):
+                    mt = b * per_bank + a
+                    nc.tensor.matmul_mx(
+                        out=acc[:, a, :],
+                        lhsT=w2_codes[:, mt * P : (mt + 1) * P].bitcast(FP8X4),
+                        lhsT_scale=w2_scales[:, mt * P : (mt + 1) * P],
+                        rhs=z_codes[:].bitcast(FP8X4),
+                        rhs_scale=z_scales[:],
+                        start=True,
+                        stop=True,
+                    )
+                res = sb.tile([P, per_bank, n], F32, name="res%d_%d" % (s0, b), align_bytes=64)
+                nc.scalar.copy(res[:], acc[:])
+                rows = out[b * per_bank * P : (b + 1) * per_bank * P, s0 : s0 + n]
+                nc.sync.dma_start(out=rows.rearrange("(a p) n -> p a n", p=P), in_=res[:])
+
+        fetch_pos(0)
+        fetch_neg(0)
+        round_w2()
+        fetch_pos(1)
+        quantize_w2()
+        fetch_pos(2)
+        losses(0)
+        fetch_neg(1)
+        losses(1)
+        second_product(0)
+        fetch_neg(2)
+        losses(2)
+        second_product(1)
+        second_product(2)

@@ -18,6 +18,8 @@ ALU = mybir.AluOpType
 P = 128
 PACK = 4
 STRIPE = 16
+BANK = 512
+HALF = S // 2
 QUARTER = S // 4
 OUT_SLICES = ((0, 256), (256, 128), (384, 128))
 
@@ -31,6 +33,9 @@ def tile_picked_focalpair_none_p_kernel(
         sb = ctx.enter_context(tc.tile_pool(name="sb", bufs=1))
         ps = ctx.enter_context(tc.psum_pool(name="ps", bufs=1))
 
+        def entries(tile, first, count):
+            return tile[:, first // STRIPE : (first + count) // STRIPE]
+
         offs_t = lists.tile([P, S // STRIPE], U16, name="offs_t")
         pos_t = lists.tile([P, S // STRIPE], U16, name="pos_t")
         neg_t = lists.tile([P, S // STRIPE], U16, name="neg_t")
@@ -38,12 +43,12 @@ def tile_picked_focalpair_none_p_kernel(
         xs_all = sb.tile([P, T], U8, name="xs_all", align_bytes=64)
         xw_all = sb.tile([P, T], U32, name="xw_all", align_bytes=64)
         w1_raw = sb.tile([P, PACK, H], F32, name="w1_raw", align_bytes=64)
-        w2_raw = sb.tile([P, PACK, N], F32, name="w2_raw", align_bytes=64)
+        w2_raw = [sb.tile([P, PACK, N // 2], F32, name="w2_raw%d" % h, align_bytes=64) for h in range(2)]
         gn_t = sb.tile([P, PACK], F32, name="gn_t", align_bytes=64)
 
         nc.vector.memset(xs_all[:].bitcast(I32), 0)
-        nc.sync.dma_start(out=w1_raw[:], in_=w1.rearrange("(p j) c -> p j c", j=PACK))
         nc.sync.dma_start(offs_t[:], offs)
+        nc.sync.dma_start(out=w1_raw[:], in_=w1.rearrange("(p j) c -> p j c", j=PACK))
         for q in range(4):
             nc.sync.dma_start(
                 out=xs_all[32 * q : 32 * q + 4, :].bitcast(I32),
@@ -53,104 +58,118 @@ def tile_picked_focalpair_none_p_kernel(
             out=xw_all[:].bitcast(I32),
             in_=x_words[0].rearrange("p n r -> p (n r)").bitcast(I32),
         )
-        nc.sync.dma_start(out=w2_raw[:], in_=w2.rearrange("(p j) c -> p j c", j=PACK))
-        nc.sync.dma_start(out=gn_t[:], in_=gn.rearrange("(p t) o -> p (t o)", t=PACK))
+        w2_rows = w2.rearrange("(p j) c -> p j c", j=PACK)
+        nc.sync.dma_start(out=w2_raw[0][:], in_=w2_rows[:, :, : N // 2])
         nc.sync.dma_start(pos_t[:], pos)
         nc.sync.dma_start(neg_t[:], neg)
+        nc.sync.dma_start(out=gn_t[:], in_=gn.rearrange("(p t) o -> p (t o)", t=PACK))
+        nc.sync.dma_start(out=w2_raw[1][:], in_=w2_rows[:, :, N // 2 :])
 
         w1_bf = sb.tile([P, PACK * H], BF16, name="w1_bf", align_bytes=64)
         w1_dst = w1_bf[:].rearrange("p (t m j) -> p m j t", t=PACK, j=PACK)
         w1_src = w1_raw[:].rearrange("p j (m t) -> p m j t", t=PACK)
-        nc.vector.tensor_copy(out=w1_dst[:, :80], in_=w1_src[:, :80])
-        nc.scalar.copy(out=w1_dst[:, 80:], in_=w1_src[:, 80:])
-        xs = [sb.tile([P, S // 2], U8, name="xs%d" % h, align_bytes=64) for h in range(2)]
-        nc.vector.tensor_copy(xs[0][:], xs_all[:].indirect(offs_t[:, : S // 2 // STRIPE]))
+        nc.vector.tensor_copy(out=w1_dst[:, :56], in_=w1_src[:, :56])
+        nc.scalar.copy(out=w1_dst[:, 56:], in_=w1_src[:, 56:])
+        xs = sb.tile([P, S], U8, name="xs", align_bytes=64)
+        nc.vector.tensor_copy(xs[:], xs_all[:].indirect(offs_t[:]))
         w1_codes = sb.tile([P, H], U32, name="w1_codes", align_bytes=64)
         w1_scales = sb.tile([P, H], U8, name="w1_scales", align_bytes=64)
         nc.vector.quantize_mx(out=w1_codes[:].bitcast(FP8X4), scales=w1_scales[:], in_=w1_bf[:])
 
         raw_p = sb.tile([P, PACK, S], F32, name="raw_p", align_bytes=64)
-        for c in range(4):
-            cols = slice(c * QUARTER, (c + 1) * QUARTER)
-            if c == 2:
-                nc.vector.tensor_copy(xs[1][:], xs_all[:].indirect(offs_t[:, S // 2 // STRIPE :]))
-            xw = sb.tile([P, QUARTER], U32, name="xw%d" % c, align_bytes=64)
-            nc.vector.tensor_copy(
-                xw[:],
-                xw_all[:].indirect(offs_t[:, c * QUARTER // STRIPE : (c + 1) * QUARTER // STRIPE]),
-            )
-            u = ps.tile([P, PACK, QUARTER], F32, name="u%d" % c)
-            for t in range(PACK):
+
+        def pick(first, count):
+            xw = sb.tile([P, count], U32, name="xw%d" % first, align_bytes=64)
+            nc.vector.tensor_copy(xw[:], xw_all[:].indirect(entries(offs_t, first, count)))
+            return xw
+
+        def first_product(bank, xw, first, count, t0):
+            tiles = BANK // count
+            u = ps.tile([P, tiles, count], F32, name="bank%d" % bank)
+            for a in range(tiles):
+                t = t0 + a
                 nc.tensor.matmul_mx(
-                    out=u[:, t, :],
+                    out=u[:, a, :],
                     lhsT=w1_codes[:, t * P : (t + 1) * P].bitcast(FP8X4),
                     lhsT_scale=w1_scales[:, t * P : (t + 1) * P],
                     rhs=xw[:].bitcast(FP8X4),
-                    rhs_scale=xs[c // 2][:, (c % 2) * QUARTER : (c % 2 + 1) * QUARTER],
+                    rhs_scale=xs[:, first : first + count],
                     start=True,
                     stop=True,
                 )
-            nc.scalar.activation(raw_p[:, :, cols], u[:], ACT.Sigmoid)
+            nc.scalar.activation(raw_p[:, t0 : t0 + tiles, first : first + count], u[:], ACT.Sigmoid)
+
+        first_product(0, pick(0, QUARTER), 0, QUARTER, 0)
+        first_product(1, pick(QUARTER, QUARTER), QUARTER, QUARTER, 0)
+        xw_rest = pick(HALF, HALF)
+        first_product(2, xw_rest, HALF, HALF, 0)
+        first_product(3, xw_rest, HALF, HALF, 2)
+
         prob = [sb.tile([P, S], F32, name="prob%d" % t, align_bytes=64) for t in range(PACK)]
         for t in range(PACK):
             nc.vector.tensor_scalar(prob[t][:], raw_p[:, t, :], 0.05, 0.95, ALU.max, ALU.min)
 
-        w2_bf = sb.tile([P, N, PACK], BF16, name="w2_bf", align_bytes=64)
+        w2_bf = [sb.tile([P, N // 2, PACK], BF16, name="w2_bf%d" % h, align_bytes=64) for h in range(2)]
         w2_codes = sb.tile([P, N], U32, name="w2_codes", align_bytes=64)
         w2_scales = sb.tile([P, N], U8, name="w2_scales", align_bytes=64)
 
-        def round_w2():
+        def round_w2(h):
             nc.vector.tensor_copy(
-                out=w2_bf[:].rearrange("p (c i) j -> p c j i", i=4),
-                in_=w2_raw[:].rearrange("p j (c i) -> p c j i", i=4),
+                out=w2_bf[h][:].rearrange("p (c i) j -> p c j i", i=4),
+                in_=w2_raw[h][:].rearrange("p j (c i) -> p c j i", i=4),
             )
 
-        def quantize_w2():
+        def quantize_w2(h):
+            cols = slice(h * N // 2, (h + 1) * N // 2)
             nc.vector.quantize_mx(
-                out=w2_codes[:].bitcast(FP8X4),
-                scales=w2_scales[:],
-                in_=w2_bf[:].rearrange("p n j -> p (n j)"),
+                out=w2_codes[:, cols].bitcast(FP8X4),
+                scales=w2_scales[:, cols],
+                in_=w2_bf[h][:].rearrange("p n j -> p (n j)"),
             )
 
-        def planes(name):
-            return [sb.tile([P, PACK, n], F32, name="%s%d" % (name, s0), align_bytes=64) for s0, n in OUT_SLICES]
+        def planes(name, slices):
+            return [sb.tile([P, PACK, n], F32, name="%s%d" % (name, s0), align_bytes=64) for s0, n in slices]
 
-        p_pos, p_neg = planes("p_pos"), planes("p_neg")
-        log_pos, log_neg = planes("log_pos"), planes("log_neg")
-        sq_pos, sq_neg = planes("sq_pos"), planes("sq_neg")
-        at_pos, at_neg = planes("at_pos"), planes("at_neg")
+        halves = ((0, HALF), (HALF, HALF))
+        p_pos, p_neg = planes("p_pos", halves), planes("p_neg", halves)
+        log_pos, log_neg = planes("log_pos", OUT_SLICES), planes("log_neg", OUT_SLICES)
+        sq_pos, sq_neg = planes("sq_pos", OUT_SLICES), planes("sq_neg", OUT_SLICES)
+        at_pos, at_neg = planes("at_pos", OUT_SLICES), planes("at_neg", OUT_SLICES)
 
-        def fetch_pos(i):
-            s0, n = OUT_SLICES[i]
+        def fetch_pos(h):
             for t in range(PACK):
-                nc.vector.tensor_copy(
-                    p_pos[i][:, t, :], prob[t][:].indirect(pos_t[:, s0 // STRIPE : (s0 + n) // STRIPE])
-                )
+                nc.vector.tensor_copy(p_pos[h][:, t, :], prob[t][:].indirect(entries(pos_t, h * HALF, HALF)))
 
-        def fetch_neg(i):
-            s0, n = OUT_SLICES[i]
+        def fetch_neg(h):
             for t in range(PACK):
-                nc.scalar.activation(
-                    p_neg[i][:, t, :],
-                    prob[t][:].indirect(neg_t[:, s0 // STRIPE : (s0 + n) // STRIPE]),
-                    ACT.Copy,
-                )
+                nc.scalar.activation(p_neg[h][:, t, :], prob[t][:].indirect(entries(neg_t, h * HALF, HALF)), ACT.Copy)
 
-        def losses(i):
-            nc.scalar.activation(log_neg[i][:], p_neg[i][:], ACT.Ln, bias=1.0, scale=-1.0)
-            nc.scalar.activation(log_pos[i][:], p_pos[i][:], ACT.Ln)
-            nc.scalar.activation(sq_pos[i][:], p_pos[i][:], ACT.Square, bias=1.0, scale=-1.0)
+        def fetched(tiles, i):
+            s0, n = OUT_SLICES[i]
+            return tiles[s0 // HALF][:, :, s0 % HALF : s0 % HALF + n]
+
+        def times_gain(dst, a, b):
             for t in range(PACK):
                 nc.vector.scalar_tensor_tensor(
-                    sq_neg[i][:, t, :], p_neg[i][:, t, :], gn_t[:, t : t + 1], p_neg[i][:, t, :], ALU.mult, ALU.mult
-                )
-            nc.vector.tensor_tensor(at_neg[i][:], sq_neg[i][:], log_neg[i][:], ALU.mult)
-            for t in range(PACK):
-                nc.vector.scalar_tensor_tensor(
-                    at_pos[i][:, t, :], sq_pos[i][:, t, :], gn_t[:, t : t + 1], log_pos[i][:, t, :], ALU.mult, ALU.mult
+                    dst[:, t, :], a[:, t, :], gn_t[:, t : t + 1], b[:, t, :], ALU.mult, ALU.mult
                 )
 
-        def second_product(i):
+        def losses(i, square_on_vector):
+            pp, pn = fetched(p_pos, i), fetched(p_neg, i)
+            if square_on_vector:
+                times_gain(sq_neg[i], pn, pn)
+            else:
+                nc.scalar.activation(sq_neg[i][:], pn, ACT.Square)
+            nc.scalar.activation(log_neg[i][:], pn, ACT.Ln, bias=1.0, scale=-1.0)
+            nc.scalar.activation(log_pos[i][:], pp, ACT.Ln)
+            nc.scalar.activation(sq_pos[i][:], pp, ACT.Square, bias=1.0, scale=-1.0)
+            if square_on_vector:
+                nc.vector.tensor_tensor(at_neg[i][:], sq_neg[i][:], log_neg[i][:], ALU.mult)
+            else:
+                times_gain(at_neg[i], sq_neg[i], log_neg[i])
+            times_gain(at_pos[i], sq_pos[i], log_pos[i])
+
+        def second_product(i, banks):
             s0, n = OUT_SLICES[i]
             z = sb.tile([P, n, PACK], BF16, name="z%d" % s0, align_bytes=64)
             nc.vector.tensor_tensor(
@@ -166,9 +185,10 @@ def tile_picked_focalpair_none_p_kernel(
                 scales=z_scales[:],
                 in_=z[:].rearrange("p n t -> p (n t)"),
             )
-            per_bank = 512 // n
-            for b in range(PACK // per_bank):
-                acc = ps.tile([P, per_bank, n], F32, name="acc%d_%d" % (s0, b))
+            per_bank = PACK // len(banks)
+            sums = []
+            for b, bank in enumerate(banks):
+                acc = ps.tile([P, per_bank, n], F32, name="bank%d" % bank)
                 for a in range(per_bank):
                     mt = b * per_bank + a
                     nc.tensor.matmul_mx(
@@ -180,22 +200,33 @@ def tile_picked_focalpair_none_p_kernel(
                         start=True,
                         stop=True,
                     )
+                sums.append(acc)
+            return sums
+
+        def store(i, sums, copies):
+            s0, n = OUT_SLICES[i]
+            per_bank = PACK // len(sums)
+            for b, (acc, copy_out) in enumerate(zip(sums, copies)):
                 res = sb.tile([P, per_bank, n], F32, name="res%d_%d" % (s0, b), align_bytes=64)
-                nc.scalar.copy(res[:], acc[:])
+                copy_out(res[:], acc[:])
                 rows = out[b * per_bank * P : (b + 1) * per_bank * P, s0 : s0 + n]
                 nc.sync.dma_start(out=rows.rearrange("(a p) n -> p a n", p=P), in_=res[:])
 
+        on_scalar, on_vector = nc.scalar.copy, nc.vector.tensor_copy
+        round_w2(0)
+        quantize_w2(0)
         fetch_pos(0)
         fetch_neg(0)
-        round_w2()
+        round_w2(1)
         fetch_pos(1)
-        quantize_w2()
-        fetch_pos(2)
-        losses(0)
+        quantize_w2(1)
+        losses(0, True)
         fetch_neg(1)
-        losses(1)
-        second_product(0)
-        fetch_neg(2)
-        losses(2)
-        second_product(1)
-        second_product(2)
+        sums0 = second_product(0, (4, 5))
+        losses(1, True)
+        losses(2, False)
+        sums1 = second_product(1, (6,))
+        sums2 = second_product(2, (7, 0))
+        store(0, sums0, (on_scalar, on_scalar))
+        store(1, sums1, (on_scalar,))
+        store(2, sums2, (on_vector, on_scalar))

@@ -107,7 +107,8 @@ def tile_picked_focalpair_none_p_kernel(
 
         prob = [sb.tile([P, S], F32, name="prob%d" % t, align_bytes=64) for t in range(PACK)]
         for t in range(PACK):
-            nc.vector.tensor_scalar(prob[t][:], raw_p[:, t, :], 0.05, 0.95, ALU.max, ALU.min)
+            engine = nc.vector if t < 2 else nc.gpsimd
+            engine.tensor_scalar(prob[t][:], raw_p[:, t, :], 0.95, 0.05, ALU.min, ALU.max)
 
         w2_bf = [sb.tile([P, N // 2, PACK], BF16, name="w2_bf%d" % h, align_bytes=64) for h in range(2)]
         w2_codes = sb.tile([P, N], U32, name="w2_codes", align_bytes=64)
@@ -140,9 +141,13 @@ def tile_picked_focalpair_none_p_kernel(
             for t in range(PACK):
                 nc.vector.tensor_copy(p_pos[h][:, t, :], prob[t][:].indirect(entries(pos_t, h * HALF, HALF)))
 
-        def fetch_neg(h):
+        def fetch_neg(h, on_vector):
             for t in range(PACK):
-                nc.scalar.activation(p_neg[h][:, t, :], prob[t][:].indirect(entries(neg_t, h * HALF, HALF)), ACT.Copy)
+                window = prob[t][:].indirect(entries(neg_t, h * HALF, HALF))
+                if t < on_vector:
+                    nc.vector.tensor_copy(p_neg[h][:, t, :], window)
+                else:
+                    nc.scalar.activation(p_neg[h][:, t, :], window, ACT.Copy)
 
         def fetched(tiles, i):
             s0, n = OUT_SLICES[i]
@@ -154,16 +159,19 @@ def tile_picked_focalpair_none_p_kernel(
                     dst[:, t, :], a[:, t, :], gn_t[:, t : t + 1], b[:, t, :], ALU.mult, ALU.mult
                 )
 
-        def losses(i, square_on_vector):
+        def losses(i, squarer):
             pp, pn = fetched(p_pos, i), fetched(p_neg, i)
-            if square_on_vector:
+            if squarer == "vector":
                 times_gain(sq_neg[i], pn, pn)
+            elif squarer == "gpsimd":
+                for t in range(PACK):
+                    nc.gpsimd.tensor_tensor(sq_neg[i][:, t, :], pn[:, t, :], pn[:, t, :], ALU.mult)
             else:
                 nc.scalar.activation(sq_neg[i][:], pn, ACT.Square)
             nc.scalar.activation(log_neg[i][:], pn, ACT.Ln, bias=1.0, scale=-1.0)
             nc.scalar.activation(log_pos[i][:], pp, ACT.Ln)
             nc.scalar.activation(sq_pos[i][:], pp, ACT.Square, bias=1.0, scale=-1.0)
-            if square_on_vector:
+            if squarer == "vector":
                 nc.vector.tensor_tensor(at_neg[i][:], sq_neg[i][:], log_neg[i][:], ALU.mult)
             else:
                 times_gain(at_neg[i], sq_neg[i], log_neg[i])
@@ -215,16 +223,16 @@ def tile_picked_focalpair_none_p_kernel(
         on_scalar, on_vector = nc.scalar.copy, nc.vector.tensor_copy
         round_w2(0)
         quantize_w2(0)
-        fetch_pos(0)
-        fetch_neg(0)
         round_w2(1)
-        fetch_pos(1)
         quantize_w2(1)
-        losses(0, True)
-        fetch_neg(1)
+        fetch_pos(0)
+        fetch_neg(0, 0)
+        fetch_pos(1)
+        losses(0, "gpsimd")
+        fetch_neg(1, 2)
         sums0 = second_product(0, (4, 5))
-        losses(1, True)
-        losses(2, False)
+        losses(1, "vector")
+        losses(2, "scalar")
         sums1 = second_product(1, (6,))
         sums2 = second_product(2, (7, 0))
         store(0, sums0, (on_scalar, on_scalar))

from contextlib import ExitStack

import concourse.mybir as mybir

K, T, S, H, N = 512, 2048, 512, 512, 512
FLOPS = 2 * K * H * S + 2 * H * N * S

F32 = mybir.dt.float32
BF16 = mybir.dt.bfloat16
I32 = mybir.dt.int32
U32 = mybir.dt.uint32
U16 = mybir.dt.uint16
U8 = mybir.dt.uint8
FP8X4 = mybir.dt.float8_e4m3fn_x4
ACT = mybir.ActivationFunctionType
ALU = mybir.AluOpType

P = 128
PACK = 4
STRIPE = 16
BANK = 512
HALF = S // 2
QUARTER = S // 4
OUT_SLICES = ((0, 256), (256, 128), (384, 128))


def tile_picked_focalpair_none_p_kernel(
    tc, x_words, x_scales, w1, gn, w2, offs, pos, neg, out
):
    nc = tc.nc
    with ExitStack() as ctx:
        lists = ctx.enter_context(tc.tile_pool(name="lists", bufs=1))
        sb = ctx.enter_context(tc.tile_pool(name="sb", bufs=1))
        ps = ctx.enter_context(tc.psum_pool(name="ps", bufs=1))

        def entries(tile, first, count):
            return tile[:, first // STRIPE : (first + count) // STRIPE]

        offs_t = lists.tile([P, S // STRIPE], U16, name="offs_t")
        pos_t = lists.tile([P, S // STRIPE], U16, name="pos_t")
        neg_t = lists.tile([P, S // STRIPE], U16, name="neg_t")

        xs_all = sb.tile([P, T], U8, name="xs_all", align_bytes=64)
        xw_all = sb.tile([P, T], U32, name="xw_all", align_bytes=64)
        w1_raw = sb.tile([P, PACK, H], F32, name="w1_raw", align_bytes=64)
        w2_raw = [sb.tile([P, PACK, N // 2], F32, name="w2_raw%d" % h, align_bytes=64) for h in range(2)]
        gn_t = sb.tile([P, PACK], F32, name="gn_t", align_bytes=64)

        nc.vector.memset(xs_all[:].bitcast(I32), 0)
        nc.sync.dma_start(offs_t[:], offs)
        nc.sync.dma_start(out=w1_raw[:], in_=w1.rearrange("(p j) c -> p j c", j=PACK))
        for q in range(4):
            nc.sync.dma_start(
                out=xs_all[32 * q : 32 * q + 4, :].bitcast(I32),
                in_=x_scales[0, 4 * q : 4 * q + 4, :].bitcast(I32),
            )
        nc.sync.dma_start(
            out=xw_all[:].bitcast(I32),
            in_=x_words[0].rearrange("p n r -> p (n r)").bitcast(I32),
        )
        w2_rows = w2.rearrange("(p j) c -> p j c", j=PACK)
        nc.sync.dma_start(out=w2_raw[0][:], in_=w2_rows[:, :, : N // 2])
        nc.sync.dma_start(pos_t[:], pos)
        nc.sync.dma_start(neg_t[:], neg)
        nc.sync.dma_start(out=gn_t[:], in_=gn.rearrange("(p t) o -> p (t o)", t=PACK))
        nc.sync.dma_start(out=w2_raw[1][:], in_=w2_rows[:, :, N // 2 :])

        w1_bf = sb.tile([P, PACK * H], BF16, name="w1_bf", align_bytes=64)
        w1_dst = w1_bf[:].rearrange("p (t m j) -> p m j t", t=PACK, j=PACK)
        w1_src = w1_raw[:].rearrange("p j (m t) -> p m j t", t=PACK)
        nc.vector.tensor_copy(out=w1_dst[:, :56], in_=w1_src[:, :56])
        nc.scalar.copy(out=w1_dst[:, 56:], in_=w1_src[:, 56:])
        xs = sb.tile([P, S], U8, name="xs", align_bytes=64)
        nc.vector.tensor_copy(xs[:], xs_all[:].indirect(offs_t[:]))
        w1_codes = sb.tile([P, H], U32, name="w1_codes", align_bytes=64)
        w1_scales = sb.tile([P, H], U8, name="w1_scales", align_bytes=64)
        nc.vector.quantize_mx(out=w1_codes[:].bitcast(FP8X4), scales=w1_scales[:], in_=w1_bf[:])

        raw_p = sb.tile([P, PACK, S], F32, name="raw_p", align_bytes=64)

        def pick(first, count):
            xw = sb.tile([P, count], U32, name="xw%d" % first, align_bytes=64)
            nc.vector.tensor_copy(xw[:], xw_all[:].indirect(entries(offs_t, first, count)))
            return xw

        def first_product(bank, xw, first, count, t0):
            tiles = BANK // count
            u = ps.tile([P, tiles, count], F32, name="bank%d" % bank)
            for a in range(tiles):
                t = t0 + a
                nc.tensor.matmul_mx(
                    out=u[:, a, :],
                    lhsT=w1_codes[:, t * P : (t + 1) * P].bitcast(FP8X4),
                    lhsT_scale=w1_scales[:, t * P : (t + 1) * P],
                    rhs=xw[:].bitcast(FP8X4),
                    rhs_scale=xs[:, first : first + count],
                    start=True,
                    stop=True,
                )
            nc.scalar.activation(raw_p[:, t0 : t0 + tiles, first : first + count], u[:], ACT.Sigmoid)

        first_product(0, pick(0, QUARTER), 0, QUARTER, 0)
        first_product(1, pick(QUARTER, QUARTER), QUARTER, QUARTER, 0)
        xw_rest = pick(HALF, HALF)
        first_product(2, xw_rest, HALF, HALF, 0)
        first_product(3, xw_rest, HALF, HALF, 2)

        prob = [sb.tile([P, S], F32, name="prob%d" % t, align_bytes=64) for t in range(PACK)]
        for t in range(PACK):
            engine = nc.vector if t < 2 else nc.gpsimd
            engine.tensor_scalar(prob[t][:], raw_p[:, t, :], 0.95, 0.05, ALU.min, ALU.max)

        w2_bf = [sb.tile([P, N // 2, PACK], BF16, name="w2_bf%d" % h, align_bytes=64) for h in range(2)]
        w2_codes = sb.tile([P, N], U32, name="w2_codes", align_bytes=64)
        w2_scales = sb.tile([P, N], U8, name="w2_scales", align_bytes=64)

        def round_w2(h):
            nc.vector.tensor_copy(
                out=w2_bf[h][:].rearrange("p (c i) j -> p c j i", i=4),
                in_=w2_raw[h][:].rearrange("p j (c i) -> p c j i", i=4),
            )

        def quantize_w2(h):
            cols = slice(h * N // 2, (h + 1) * N // 2)
            nc.vector.quantize_mx(
                out=w2_codes[:, cols].bitcast(FP8X4),
                scales=w2_scales[:, cols],
                in_=w2_bf[h][:].rearrange("p n j -> p (n j)"),
            )

        def planes(name, slices):
            return [sb.tile([P, PACK, n], F32, name="%s%d" % (name, s0), align_bytes=64) for s0, n in slices]

        halves = ((0, HALF), (HALF, HALF))
        p_pos, p_neg = planes("p_pos", halves), planes("p_neg", halves)
        log_pos, log_neg = planes("log_pos", OUT_SLICES), planes("log_neg", OUT_SLICES)
        sq_pos, sq_neg = planes("sq_pos", OUT_SLICES), planes("sq_neg", OUT_SLICES)
        at_pos, at_neg = planes("at_pos", OUT_SLICES), planes("at_neg", OUT_SLICES)

        def fetch_pos(h):
            for t in range(PACK):
                nc.vector.tensor_copy(p_pos[h][:, t, :], prob[t][:].indirect(entries(pos_t, h * HALF, HALF)))

        def fetch_neg(h, on_vector):
            for t in range(PACK):
                window = prob[t][:].indirect(entries(neg_t, h * HALF, HALF))
                if t < on_vector:
                    nc.vector.tensor_copy(p_neg[h][:, t, :], window)
                else:
                    nc.scalar.activation(p_neg[h][:, t, :], window, ACT.Copy)

        def fetched(tiles, i):
            s0, n = OUT_SLICES[i]
            return tiles[s0 // HALF][:, :, s0 % HALF : s0 % HALF + n]

        def times_gain(dst, a, b):
            for t in range(PACK):
                nc.vector.scalar_tensor_tensor(
                    dst[:, t, :], a[:, t, :], gn_t[:, t : t + 1], b[:, t, :], ALU.mult, ALU.mult
                )

        def losses(i, squarer):
            pp, pn = fetched(p_pos, i), fetched(p_neg, i)
            if squarer == "vector":
                times_gain(sq_neg[i], pn, pn)
            elif squarer == "gpsimd":
                for t in range(PACK):
                    nc.gpsimd.tensor_tensor(sq_neg[i][:, t, :], pn[:, t, :], pn[:, t, :], ALU.mult)
            else:
                nc.scalar.activation(sq_neg[i][:], pn, ACT.Square)
            nc.scalar.activation(log_neg[i][:], pn, ACT.Ln, bias=1.0, scale=-1.0)
            nc.scalar.activation(log_pos[i][:], pp, ACT.Ln)
            nc.scalar.activation(sq_pos[i][:], pp, ACT.Square, bias=1.0, scale=-1.0)
            if squarer == "vector":
                nc.vector.tensor_tensor(at_neg[i][:], sq_neg[i][:], log_neg[i][:], ALU.mult)
            else:
                times_gain(at_neg[i], sq_neg[i], log_neg[i])
            times_gain(at_pos[i], sq_pos[i], log_pos[i])

        def second_product(i, banks):
            s0, n = OUT_SLICES[i]
            z = sb.tile([P, n, PACK], BF16, name="z%d" % s0, align_bytes=64)
            nc.vector.tensor_tensor(
                z[:].rearrange("p (c i) t -> p c t i", i=2),
                at_neg[i][:].rearrange("p t (c i) -> p c t i", i=2),
                at_pos[i][:].rearrange("p t (c i) -> p c t i", i=2),
                ALU.subtract,
            )
            z_codes = sb.tile([P, n], U32, name="z_codes%d" % s0, align_bytes=64)
            z_scales = sb.tile([P, n], U8, name="z_scales%d" % s0, align_bytes=64)
            nc.vector.quantize_mx(
                out=z_codes[:].bitcast(FP8X4),
                scales=z_scales[:],
                in_=z[:].rearrange("p n t -> p (n t)"),
            )
            per_bank = PACK // len(banks)
            sums = []
            for b, bank in enumerate(banks):
                acc = ps.tile([P, per_bank, n], F32, name="bank%d" % bank)
                for a in range(per_bank):
                    mt = b * per_bank + a
                    nc.tensor.matmul_mx(
                        out=acc[:, a, :],
                        lhsT=w2_codes[:, mt * P : (mt + 1) * P].bitcast(FP8X4),
                        lhsT_scale=w2_scales[:, mt * P : (mt + 1) * P],
                        rhs=z_codes[:].bitcast(FP8X4),
                        rhs_scale=z_scales[:],
                        start=True,
                        stop=True,
                    )
                sums.append(acc)
            return sums

        def store(i, sums, copies):
            s0, n = OUT_SLICES[i]
            per_bank = PACK // len(sums)
            for b, (acc, copy_out) in enumerate(zip(sums, copies)):
                res = sb.tile([P, per_bank, n], F32, name="res%d_%d" % (s0, b), align_bytes=64)
                copy_out(res[:], acc[:])
                rows = out[b * per_bank * P : (b + 1) * per_bank * P, s0 : s0 + n]
                nc.sync.dma_start(out=rows.rearrange("(a p) n -> p a n", p=P), in_=res[:])

        on_scalar, on_vector = nc.scalar.copy, nc.vector.tensor_copy
        round_w2(0)
        quantize_w2(0)
        round_w2(1)
        quantize_w2(1)
        fetch_pos(0)
        fetch_neg(0, 0)
        fetch_pos(1)
        losses(0, "gpsimd")
        fetch_neg(1, 2)
        sums0 = second_product(0, (4, 5))
        losses(1, "vector")
        losses(2, "scalar")
        sums1 = second_product(1, (6,))
        sums2 = second_product(2, (7, 0))
        store(0, sums0, (on_scalar, on_scalar))
        store(1, sums1, (on_scalar,))
        store(2, sums2, (on_vector, on_scalar))
